import numpy as np
CORES = [33,34,161,162,289,290,417,418]
N = 8
R, T, B = 4096, 2048, 256
def entries(a): return a.T.reshape(-1)
def pack(v, P): return np.ascontiguousarray(np.asarray(v, np.int32).reshape(-1, P).T)
def lists(rng, how):
    I = rng.integers(0, N * R, (N, T)); E = np.sort(rng.integers(0, T + 1, (N, B)), axis=1)
    if how == "void":
        E = np.zeros((N, B), np.int64)
        for r in range(N): k = np.sort(1 + rng.permutation(B - 2)[:6]); c = np.sort(1 + rng.permutation(T)[:6]); E[r] = np.concatenate([[0], c])[np.searchsorted(k, np.arange(B), side="right")]
        E[rng.integers(N)] = 0
    if how == "one":
        p = rng.permutation(N); z = rng.integers(0, B, N); z[p[0]] = 0; z[p[1]] = B - 1; E = np.where(np.arange(B)[None, :] < z[:, None], 0, T)
        I[p[::2]] = R * p[1] + I[p[::2]] % R
    if how == "single": E = np.broadcast_to(1 + np.arange(B), (N, B)).copy()
    if how == "hotrank": I = R * int(rng.integers(N)) + rng.integers(0, R, (N, T))
    if how == "edge": I = R * rng.integers(0, N, (N, T)) + np.where(rng.random((N, T)) < 0.5, 0, R - 1); E[:, -1] = T
    return {"idx": np.stack([pack(i, 16) for i in I]), "end": np.stack([pack(v, 16) for v in E])}
def setup_inputs(rng):
    return dict({"tab": rng.standard_normal((N, 128, R), dtype=np.float32)}, **lists(rng, "uniform"))
def setup_inputs_edge(rng):
    d = setup_inputs(rng); d.update(lists(rng, "edge"))
    for k in ("tab",): d[k] = (d[k].astype(np.float32) * 1048576.0).astype(d[k].dtype)
    return d
def setup_inputs_hotrank(rng):
    d = setup_inputs(rng); d.update(lists(rng, "hotrank"))
    for k in ("tab",): d[k] = (d[k].astype(np.float32) * (1 / 1024.0)).astype(d[k].dtype)
    return d
def setup_inputs_one(rng):
    d = setup_inputs(rng); d.update(lists(rng, "one"))
    return d
def setup_inputs_single(rng):
    d = setup_inputs(rng); d.update(lists(rng, "single"))
    return d
def setup_inputs_void(rng):
    d = setup_inputs(rng); d.update(lists(rng, "void"))
    return d
def check_inputs(x):
    bad = []
    if x["idx"].min() < 0 or x["idx"].max() >= N * R: bad.append("idx out of range")
    if x["end"].min() < 0 or x["end"].max() >= T + 1: bad.append("end out of range")
    if any((np.diff(entries(a)) < 0).any() for a in x["end"]): bad.append("end falls")
    t = x["tab"].astype(np.float32)
    if t.min() < -1e30 or t.max() > 1e30: bad.append("tab beyond -1e30 to 1e30")
    return bad
def reference(tab, idx, end):
    A = np.concatenate(list(tab), axis=1)
    y = np.zeros((N, 128, B), tab.dtype)
    for r in range(N):
        G = A[:, entries(idx[r])]; c = np.concatenate([[0], entries(end[r])])
        for b in range(B):
            if c[b + 1] > c[b]: y[r][:, b] = G[:, c[b]:c[b + 1]].max(axis=1)
    return {"y": y}

@@ -1,0 +1,434 @@
+from concourse.bass import DstId, RemoteDMATransfer
+from concourse.mybir import AluOpType as A, ActivationFunctionType as AF
+
+N, R, TL, B = 8, 4096, 2048, 256
+ALL = 512
+G = 4
+W = R + 2 * G
+H, Q = TL // 2, TL // 4
+SW = TL + 4
+OW = 144
+MW = 160
+NCH = 8
+NL = 8
+DEEP = 3
+EARLY = 2
+NG = 4
+
+WHO = {("own", 0): "o", ("own", 1): "o", ("chip", 0): "h3", ("chip", 1): "h3", ("rack", 0): "h1", ("rack", 1): "h2", ("cable", 0): "o", ("cable", 1): "h1", ("diag", 0): "o", ("diag", 1): "o"}
+ORDER = {"o": [("own", 0), ("own", 1), ("diag", 0), ("diag", 1), ("cable", 0)], "h1": [("cable", 1), ("rack", 0)], "h2": [("rack", 1)], "h3": [("chip", 0), ("chip", 1)]}
+RELAY = ["h3", "h3"]
+REST = [[("diag", 0), ("diag", 1), ("cable", 0), ("cable", 1), ("rack", 0), ("rack", 1), ("chip", 0), ("chip", 1)]] * 2
+
+SCRATCH = {
+    "win": ("sbuf", [128, W], "float32"),
+    "gv": ("sbuf", [128, Q], "float32"),
+    "sc0": ("sbuf", [128, SW], "float32"),
+    "sc1": ("sbuf", [128, SW], "float32"),
+    "sco": ("sbuf", [128, SW], "float32"),
+    "res": ("sbuf", [128, N * B], "float32"),
+    "land": ("sbuf", [128, N * B], "float32"),
+    "yb": ("sbuf", [128, B], "float32"),
+    "offs": ("sbuf", [128, N * OW], "uint16"),
+    "ix": ("sbuf", [128, N * 128], "int32"),
+    "cl": ("sbuf", [128, N * 128], "float32"),
+    "mm": ("sbuf", [128, N * MW], "bfloat16"),
+    "ones": ("sbuf", [128, 128], "float32"),
+    "cst": ("sbuf", [128, 128], "bfloat16"),
+    "iot": ("sbuf", [128, 128], "float32"),
+    "idn": ("sbuf", [128, 16], "float32"),
+    "repf": ("sbuf", [128, 128], "float32"),
+    "rep1": ("sbuf", [128, 128], "bfloat16"),
+    "rep16": ("sbuf", [128, 128], "bfloat16"),
+    "sel": ("sbuf", [128, TL], "bfloat16"),
+    "low": ("sbuf", [128, 4], "float32"),
+    "e2": ("sbuf", [128, 2], "int32"),
+    "hl": ("sbuf", [128, 4], "int32"),
+    "hlf": ("sbuf", [128, 4], "float32"),
+    "oh": ("sbuf", [128, 2 * OW], "bfloat16"),
+    "ei": ("sbuf", [128, 16], "int32"),
+    "pv": ("sbuf", [128, 16], "int32"),
+    "ne": ("sbuf", [128, 16], "float32"),
+    "eu": ("sbuf", [128, 16], "float32"),
+    "ew": ("sbuf", [128, 16], "float32"),
+    "exi": ("sbuf", [128, 16], "int32"),
+    "xh": ("sbuf", [128, 32], "int32"),
+    "m1": ("dram", [128, 16], "int32"),
+    "m2": ("dram", [128, 20], "bfloat16"),
+    "L1": ("dram", [N, 128, 16], "int32"),
+    "L2": ("dram", [N, 128, 20], "bfloat16"),
+    "mk0": ("psum", [128, H], "float32"),
+    "mk1": ("psum", [128, H], "float32"),
+    "mk2": ("psum", [128, H], "float32"),
+    "rp": ("psum", [128, 512], "float32"),
+    "ex": ("psum", [128, 512], "float32"),
+}
+for _k in range(NG): SCRATCH["gb%d" % _k] = ("sbuf", [128, H], "float32")
+SEMAPHORES = (["sv", "ss", "st", "sg", "dm1", "dm2", "de", "dp", "snt", "sw0", "sw1", "dy"]
+              + ["tb%d" % k for k in range(DEEP)] + ["tw%d" % k for k in range(NCH)]
+              + ["%s_%d" % (n, t) for n in ("a1", "a2", "d1", "d2", "r") for t in range(N)])
+
+
+def bits(m):
+    return bin(m).count("1")
+
+
+def the_plan(cores, topo):
+    key = lambda c: (topo.host(c), topo.chip(c))
+    chips = {}
+    for c in range(ALL):
+        chips.setdefault(key(c), []).append(c)
+    mates = [[s for s in range(N) if key(cores[s]) == key(cores[t])] for t in range(N)]
+    pos = [mates[t].index(t) for t in range(N)]
+
+    def rel(s, t):
+        a, b = cores[s], cores[t]
+        if s == t: return "own"
+        if key(a) == key(b): return "chip"
+        if topo.host(a) != topo.host(b) and not topo.may_write(a, b): return "diag"
+        return "rack" if topo.rack(topo.host(a)) == topo.rack(topo.host(b)) else "cable"
+
+    team = []
+    for s in range(N):
+        free = [c for c in chips[key(cores[s])] if c not in cores]
+        near = [c for c in free if topo.die(c) == topo.die(cores[s])]
+        far = [c for c in free if topo.die(c) != topo.die(cores[s])]
+        team.append({"o": cores[s], "h1": near[pos[s]], "h2": far[2 * pos[s]], "h3": far[2 * pos[s] + 1]})
+    relay = []
+    for t in range(N):
+        across = [s for s in range(N) if rel(s, t) == "cable"]
+        relay.append(team[across[pos[t]]][RELAY[pos[t]]])
+    todo, proc = {}, {}
+    for s in range(N):
+        for role in team[s]:
+            lists = [t for k in ORDER[role] for t in range(N) if (rel(s, t), pos[t]) == k and WHO[k] == role]
+            todo[team[s][role]] = (s, lists)
+            for t in lists: proc[(s, t)] = team[s][role]
+
+    def mask_of(src, dsts):
+        m = topo.mask(src, dsts[0])
+        for d in dsts: m &= topo.mask(src, d)
+        return m
+
+    edges = []
+    for m in (1, 2):
+        for t in range(N):
+            direct, later = [], []
+            for k in ("cable", "rack", "chip"):
+                pair = [proc[(s, t)] for s in range(N) if rel(s, t) == k]
+                if len(pair) == 1 or pair[0] in cores:
+                    direct += pair
+                else:
+                    i = (m + (k == "rack")) % 2
+                    direct.append(pair[i])
+                    later.append((m, t, pair[i], [pair[1 - i]]))
+            if relay[t] not in direct: direct.append(relay[t])
+            later.append((m, t, relay[t], [proc[(s, t)] for s in range(N) if rel(s, t) == "diag"]))
+            edges.append((m, t, cores[t], direct))
+            edges += later
+    return dict(rel=rel, pos=pos, team=team, relay=relay, todo=todo, proc=proc, edges=edges, mask_of=mask_of)
+
+
+PLANS = {}
+
+
+def rank_program(g, core, T, topo):
+    cores = list(T.cores)
+    if "p" not in PLANS: PLANS["p"] = the_plan(cores, topo)
+    P = PLANS["p"]
+    if core not in P["todo"]: return
+    rel, relay, proc, mask_of = P["rel"], P["relay"], P["proc"], P["mask_of"]
+    me = T.rank_of(core)
+    V, S, E, Y = g.vector, g.scalar, g.tensor, g.sync
+    cnt, seen, top = {}, {}, {}
+
+    def due(sem, n):
+        cnt[sem] = cnt.get(sem, 0) + n
+        return (sem, cnt[sem])
+
+    def wait(q, *toks):
+        best = {}
+        for k in toks:
+            if k is not None: best[k[0]] = max(best.get(k[0], 0), k[1])
+        name = "V" if q is V else "S" if q is S else "E" if q is E else "Y" if q is Y else "g"
+        for sem in best:
+            v = best[sem]
+            if seen.get((name, sem), 0) < v:
+                q.wait_ge(T.sem[sem], v)
+                seen[(name, sem)] = v
+                top[sem] = max(top.get(sem, 0), v)
+
+    def did(ins, sem, n=1):
+        ins.then_inc(T.sem[sem], n)
+        return due(sem, n)
+
+    def ids(dsts):
+        out = []
+        for d in dsts:
+            rid, pid = topo.addr(d, core)
+            out.append(DstId(rid=rid, pnc=pid))
+        return out
+
+    def send(dsts, srcs, dst, sem, local="snt", op=0):
+        m = mask_of(core, dsts)
+        g.remote_dma_fused([RemoteDMATransfer(dst_ids=ids(dsts), dma_engine_mask=m, remote_sem=T.sem[sem],
+                                              srcs=srcs, dsts=[dst for d in dsts], alu_op=op)], local_sem=T.sem[local])
+        return due(local, bits(m))
+
+    def finish():
+        for sem in cnt:
+            if top.get(sem, 0) < cnt[sem]: wait(g, (sem, cnt[sem]))
+
+    def blk(buf, t, w=B):
+        return T[buf][:, t * w:(t + 1) * w]
+
+    part, lists = P["todo"][core]
+    team = P["team"][part]
+    chain = [team[k] for k in ("o", "h1", "h2", "h3") if P["todo"][team[k]][1]]
+    here = chain.index(core) if core in chain else len(chain)
+    nxt = chain[here + 1] if here + 1 < len(chain) else None
+    arr = {}
+    for m, t, src, dsts in P["edges"]:
+        if core in dsts: arr[(m, t)] = due("a%d_%d" % (m, t), bits(mask_of(src, dsts)))
+
+    d1, d2, tab = {}, {}, []
+    if me is not None:
+        pv0 = did(V.memset(T.pv[0:16, :], 0), "sv")
+        de = did(S.dma_start(out=T.e2[:], in_=T.end[:]), "de", 16)
+        dm1 = did(Y.dma_start(out=T.m1[:], in_=T.idx[:]), "dm1", 16)
+        did(Y.dma_start(out=T.ei[0:16, :], in_=T.end[:]), "dp", 16)
+        wait(Y, pv0)
+        did(Y.dma_start(out=T.pv[1:16, :], in_=T.end[0:15, :]), "dp", 16)
+        dp = did(Y.dma_start(out=T.pv[0:1, 1:16], in_=T.end[15:16, 0:15]), "dp", 16)
+        d1[me] = did(Y.dma_start(out=T.ix[0:16, me * 128:(me + 1) * 128], in_=T.idx[:]), "d1_%d" % me, 16)
+        w, q = 128 // NL, R // NCH
+        tab.append(did(S.dma_start(out=T.win[:, G:G + q], in_=T.tab[:, 0:q]), "tb0", 16))
+        for k in range(NL):
+            if k >= DEEP - 1: wait(S, tab[k + 1 - DEEP])
+            tab.append(did(S.dma_start(out=T.win[k * w:(k + 1) * w, G + q:G + R], in_=T.tab[k * w:(k + 1) * w, q:R]),
+                           "tb%d" % ((k + 1) % DEEP), 16))
+    elif lists:
+        tab = [due("tw%d" % k, bits(topo.mask(chain[here - 1], core))) for k in range(NCH)]
+
+    if lists:
+        k1 = did(V.memset(T.ones[:], 1.0), "sv")
+        k2 = did(V.memset(T.cst[:], 1048576.0), "sv")
+        low = did(V.memset(T.low[:], -9e29), "sv")
+        did(V.memset(T.sco[:, TL:SW], 0.0), "sv")
+        if me is not None: kio = did(g.iota(T.iot[:], [[1, 128]], 0, 0, allow_small_or_imprecise_dtypes=True), "sg")
+        wait(g, k1)
+        kid = did(g.affine_select(T.idn[0:16, :], T.ones[0:16, 0:16], [[1, 16]], A.is_equal, 0.0, 0, -1), "sg")
+        krf = did(g.affine_select(T.repf[0:16, :], T.ones[0:16, :], [[0, 8], [1, 16]], A.is_equal, 0.0, 0, -1), "sg")
+
+    edges = [e for e in P["edges"] if e[2] == core]
+    exfree = None
+    if me is not None:
+        wait(g, dm1)
+        send(edges[0][3], [T.m1[:]], T.L1[me], "a1_%d" % me)
+        wait(V, de)
+        did(V.tensor_scalar(T.hl[:, 0:2], T.e2[:], 7, None, A.arith_shift_right), "sv")
+        k = did(V.tensor_scalar(T.hl[:, 2:4], T.e2[:], 127, None, A.bitwise_and), "sv")
+        wait(V, k)
+        k = did(V.tensor_copy(T.hlf[:], T.hl[:]), "sv")
+        wait(V, k, kio)
+        for h in range(2):
+            o = h * OW
+            did(V.tensor_scalar(T.oh[:, o:o + 16], T.iot[:, 0:16], T.hlf[:, h:h + 1], None, A.is_equal), "sv")
+            k = did(V.tensor_scalar(T.oh[:, o + 16:o + OW], T.iot[:], T.hlf[:, 2 + h:3 + h], None, A.is_equal), "sv")
+        wait(E, k)
+        for h in range(2):
+            o = h * OW
+            kf = did(E.matmul(T.ex[0:16, 0:128], T.oh[:, o:o + 16], T.oh[:, o + 16:o + OW], h == 0, h == 1), "st")
+        wait(V, dp)
+        did(V.tensor_tensor(T.ne[0:16, :], T.ei[0:16, :], T.pv[0:16, :], A.is_gt), "sv")
+        k = did(V.tensor_scalar(T.eu[0:16, :], T.ei[0:16, :], float(-1 - TL), None, A.add), "sv")
+        wait(V, k)
+        k = did(V.tensor_tensor(T.ew[0:16, :], T.eu[0:16, :], T.ne[0:16, :], A.mult), "sv")
+        wait(V, k)
+        k = did(V.tensor_scalar(T.exi[0:16, :], T.ew[0:16, :], float(TL), None, A.add), "sv")
+        wait(V, k)
+        did(V.tensor_scalar(T.xh[0:16, 0:16], T.exi[0:16, :], 4, None, A.arith_shift_right), "sv")
+        k = did(V.tensor_scalar(T.xh[0:16, 16:32], T.exi[0:16, :], 15, None, A.bitwise_and), "sv")
+        wait(V, k)
+        o = me * MW
+        did(V.tensor_copy(T.mm[0:16, o + 128:o + MW], T.xh[0:16, :]), "sv")
+        wait(V, kf)
+        k = did(V.tensor_scalar(T.mm[0:16, o:o + 128], T.ex[0:16, 0:128], -2.0 ** 90, 2.0 ** 89, A.mult, A.add), "sv")
+        exfree = d2[me] = k
+        wait(Y, k)
+        k = did(Y.dma_start(out=T.m2[:], in_=T.mm[0:16, o:o + MW]), "dm2", 16)
+        wait(g, k)
+        send(edges[1][3], [T.m2[:]], T.L2[me], "a2_%d" % me)
+    else:
+        for m, t, src, dsts in edges:
+            wait(g, arr[(m, t)])
+            L = (T.L1, T.L2)[m - 1]
+            send(dsts, [L[t]], L[t], "a%d_%d" % (m, t))
+    if nxt is not None:
+        sw, w = [None, None], R // NCH
+        for k in range(NCH):
+            if me is None: wait(g, tab[k])
+            elif k == 0: wait(g, *tab[:len(tab) - EARLY])
+            else: wait(g, *tab)
+            wait(g, sw[k % 2])
+            piece = T.win[:, G + k * w:G + (k + 1) * w]
+            sw[k % 2] = send([nxt], [piece], piece, "tw%d" % k, "sw%d" % (k % 2))
+    for t in range(N):
+        if relay[t] != core: continue
+        ss = [s for s in range(N) if rel(s, t) == "diag"]
+        wait(g, *[due("r_%d" % s, bits(topo.mask(proc[(s, t)], core))) for s in ss])
+        send([cores[t]], [blk("land", s) for s in ss], blk("land", ss[0]), "r_%d" % ss[0], op=2)
+    if not lists: return finish()
+
+    for some in ([t for t in lists if rel(part, t) != "diag"], [t for t in lists if rel(part, t) == "diag"]):
+        for m, L, d, dst, w in ((1, T.L1, d1, "ix", 128), (2, T.L2, d2, "mm", MW)):
+            for t in some:
+                if t == me: continue
+                wait(Y, arr[(m, t)])
+                d[t] = did(Y.dma_start(out=T[dst][0:16, t * w:(t + 1) * w], in_=L[t]), "d%d_%d" % (m, t), 16)
+
+    wait(V, low)
+    for ap in (T.win[:, 0:G], T.win[:, G + R:W], T.sc0[:, TL:SW], T.sc1[:, TL:SW]):
+        kgd = did(V.tensor_scalar(ap, T.low[:], 4.0, None, A.mult), "sv")
+    wait(V, k2, kid, krf)
+    did(V.tensor_copy(T.rep1[0:16, :], T.repf[0:16, :]), "sv")
+    krp = did(V.tensor_scalar(T.rep16[0:16, :], T.repf[0:16, :], 16.0, None, A.mult), "sv")
+    ksel = None
+
+    n = len(lists)
+    vl = 0 if me is not None else min(n - 1, 1)
+    steps = []
+    for i in range(n):
+        if i == vl or i == n - 1: steps += [(i, 0, H), (i, H, Q), (i, H + Q, Q)]
+        else: steps += [(i, 0, H), (i, H, H)]
+    vstep = steps.index((vl, H + Q, Q))
+    first = [min(k for k in range(len(steps)) if steps[k][0] == i) for i in range(n)]
+    final = [max(k for k in range(len(steps)) if steps[k][0] == i) for i in range(n)]
+    mk = [T.mk0, T.mk1, T.mk2]
+    free = {"rp": None, "ex": exfree}
+    v1, e1, v2, e2, v3, mtok, gtok, stok, scfree = {}, {}, {}, {}, {}, {}, {}, {}, {}
+
+    def V1(i):
+        t = lists[i]
+        wait(V, d1[t])
+        v1[i] = did(V.tensor_scalar(T.cl[0:16, t * 128:(t + 1) * 128], T.ix[0:16, t * 128:(t + 1) * 128],
+                                    float(G - R * part), float(G + R), A.add, A.min), "sv")
+
+    def E1(i):
+        t = lists[i]
+        wait(E, v1[i], krf, free["rp"])
+        e1[i] = did(E.matmul(T.rp[:, 0:128], T.repf[0:16, :], T.cl[0:16, t * 128:(t + 1) * 128], True, True), "st")
+
+    def V2(i):
+        t = lists[i]
+        wait(V, e1[i])
+        v2[i] = free["rp"] = did(V.tensor_copy(T.offs[:, t * OW:t * OW + 128], T.rp[:, 0:128]), "sv")
+
+    def E2(i):
+        o = lists[i] * MW
+        wait(E, d2[lists[i]], krp, free["ex"])
+        did(E.matmul(T.ex[:, 0:16], T.rep16[0:16, :], T.mm[0:16, o + 128:o + 144], True, False), "st")
+        e2[i] = did(E.matmul(T.ex[:, 0:16], T.rep1[0:16, :], T.mm[0:16, o + 144:o + 160], False, True), "st")
+
+    def V3(i):
+        o = lists[i] * OW
+        wait(V, e2[i])
+        v3[i] = free["ex"] = did(V.tensor_copy(T.offs[:, o + 128:o + OW], T.ex[:, 0:16]), "sv")
+
+    def M(k):
+        i, a, w = steps[k]
+        o = lists[i] * MW
+        wait(E, d2[lists[i]], ksel, stok.get(k - 3))
+        for h in range(w // 128):
+            hh = a // 128 + h
+            mtok[k] = did(E.matmul(mk[k % 3][:, h * 128:(h + 1) * 128], T.sel[0:16, hh * 128:(hh + 1) * 128],
+                                   T.mm[0:16, o:o + 128], True, True), "st")
+
+    def gathered(k):
+        return T.gv if k == vstep else T["gb%d" % (k % NG)]
+
+    def gather(k):
+        i, a, w = steps[k]
+        o = lists[i] * OW + a // 16
+        from_win = T.win[:, :].indirect(T.offs[:, o:o + w // 16])
+        if k == vstep:
+            wait(V, v2[i], kgd, *tab)
+            gtok[k] = did(V.tensor_copy(T.gv[:, 0:w], from_win), "sv")
+        else:
+            wait(S, v2[i], kgd, stok.get(k - NG), *tab)
+            gtok[k] = did(S.activation(gathered(k)[:, 0:w], from_win, AF.Copy), "ss")
+
+    def scbuf(i):
+        return "sco" if lists[i] == part else "sc%d" % (i % 2)
+
+    def scan(k):
+        i, a, w = steps[k]
+        sc = T[scbuf(i)]
+        before = [stok[j] for j in range(k) if steps[j][0] == i][-1:]
+        wait(V, mtok[k], gtok[k], kgd, scfree.get(scbuf(i)), *before)
+        init = sc[:, a - 1:a] if a else T.win[:, 0:1]
+        stok[k] = did(V.tensor_tensor_scan(sc[:, a:a + w], mk[k % 3][:, 0:w], gathered(k)[:, 0:w], init, A.min, A.max), "sv")
+
+    def picked(i):
+        o = lists[i] * OW
+        return T[scbuf(i)][:, :].indirect(T.offs[:, o + 128:o + OW])
+
+    def ext(i):
+        t = lists[i]
+        wait(V, stok[final[i]], v3[i])
+        k = did(V.tensor_copy(blk("res", t), picked(i)), "sv")
+        scfree[scbuf(i)] = k
+        if t == me: return k
+        dest = relay[t] if rel(part, t) == "diag" else cores[t]
+        wait(g, k)
+        return send([dest], [blk("res", t)], blk("land", part), "r_%d" % part)
+
+    V1(0)
+    E1(0)
+    V2(0)
+    for h in range(16):
+        ksel = did(V.tensor_scalar(T.sel[0:16, h * 128:(h + 1) * 128], T.cst[0:16, :], T.idn[0:16, h:h + 1], None, A.mult), "sv")
+    gather(0)
+    M(0)
+    E2(0)
+    V3(0)
+    if vl == 0: gather(vstep)
+    if n > 1:
+        V1(1)
+        E1(1)
+        V2(1)
+    if vl == 1: gather(vstep)
+    ahead, own = 1, None
+    for k in range(len(steps)):
+        i = steps[k][0]
+        while ahead < len(steps) and ahead <= k + 2 and steps[ahead][0] in v2:
+            if ahead != vstep: gather(ahead)
+            M(ahead)
+            if ahead == first[steps[ahead][0]]: E2(steps[ahead][0])
+            ahead += 1
+        later = i + 1 if k == first[i] and i >= 1 and i + 1 < n else None
+        if later is not None:
+            V1(later)
+            E1(later)
+        scan(k)
+        if later is not None: V2(later)
+        if k == first[i] and i > 0: V3(i)
+        if k == final[i]:
+            x = ext(i)
+            if lists[i] == me: own = x
+
+    if me is not None:
+        came = {}
+        for s in range(N):
+            if s != me and rel(s, me) != "diag": came[s] = due("r_%d" % s, bits(topo.mask(proc[(s, me)], core)))
+        s0 = [s for s in range(N) if rel(s, me) == "diag"][0]
+        came[s0] = due("r_%d" % s0, bits(topo.mask(relay[me], core)))
+        acc, ak = T.ex[:, 0:B], own
+        rest = sorted(came, key=lambda s: REST[P["pos"][me]].index((rel(s, me), P["pos"][s])))
+        for s in rest:
+            wait(V, ak, came[s], free["ex"])
+            ak = did(V.tensor_tensor(T.yb[:] if s == rest[-1] else acc, blk("land", s), blk("res", me) if s == rest[0] else acc,
+                                     A.max), "sv")
+        wait(Y, ak)
+        did(Y.dma_start(out=T.y[:], in_=T.yb[:]), "dy", 16)
+    finish()

@@ -9,16 +9,15 @@ H, Q = TL // 2, TL // 4
 SW = TL + 4
 OW = 144
 MW = 160
-NCH = 8
+NCH = 4
 NL = 8
 DEEP = 3
-EARLY = 2
+EARLY = 3
 NG = 4
 
-WHO = {("own", 0): "o", ("own", 1): "o", ("chip", 0): "h3", ("chip", 1): "h3", ("rack", 0): "h1", ("rack", 1): "h2", ("cable", 0): "o", ("cable", 1): "h1", ("diag", 0): "o", ("diag", 1): "o"}
-ORDER = {"o": [("own", 0), ("own", 1), ("diag", 0), ("diag", 1), ("cable", 0)], "h1": [("cable", 1), ("rack", 0)], "h2": [("rack", 1)], "h3": [("chip", 0), ("chip", 1)]}
-RELAY = ["h3", "h3"]
-REST = [[("diag", 0), ("diag", 1), ("cable", 0), ("cable", 1), ("rack", 0), ("rack", 1), ("chip", 0), ("chip", 1)]] * 2
+ORDER = {"o": [("own", 0), ("own", 1), ("diag", 0), ("diag", 1), ("cable", 0)],
+         "h1": [("cable", 1), ("rack", 0), ("chip", 0), ("chip", 1)], "h2": [("rack", 1)], "h3": []}
+REST = [["diag", "rack", "cable", "chip"], ["cable", "rack", "diag", "chip"]]
 
 SCRATCH = {
     "win": ("sbuf", [128, W], "float32"),
@@ -94,14 +93,16 @@ def the_plan(cores, topo):
         near = [c for c in free if topo.die(c) == topo.die(cores[s])]
         far = [c for c in free if topo.die(c) != topo.die(cores[s])]
         team.append({"o": cores[s], "h1": near[pos[s]], "h2": far[2 * pos[s]], "h3": far[2 * pos[s] + 1]})
-    relay = []
+    relay, via = [], [[], []]
     for t in range(N):
-        across = [s for s in range(N) if rel(s, t) == "cable"]
-        relay.append(team[across[pos[t]]][RELAY[pos[t]]])
+        across = team[[s for s in range(N) if rel(s, t) == "cable"][pos[t]]]
+        relay.append(across["h3"])
+        via[0].append(across["o"])
+        via[1].append(across["h3"])
     todo, proc = {}, {}
     for s in range(N):
         for role in team[s]:
-            lists = [t for k in ORDER[role] for t in range(N) if (rel(s, t), pos[t]) == k and WHO[k] == role]
+            lists = [t for k in ORDER[role] for t in range(N) if (rel(s, t), pos[t]) == k]
             todo[team[s][role]] = (s, lists)
             for t in lists: proc[(s, t)] = team[s][role]
 
@@ -122,8 +123,9 @@ def the_plan(cores, topo):
                     i = (m + (k == "rack")) % 2
                     direct.append(pair[i])
                     later.append((m, t, pair[i], [pair[1 - i]]))
-            if relay[t] not in direct: direct.append(relay[t])
-            later.append((m, t, relay[t], [proc[(s, t)] for s in range(N) if rel(s, t) == "diag"]))
+            v = via[m - 1][t]
+            if v not in direct: direct.append(v)
+            later.append((m, t, v, [proc[(s, t)] for s in range(N) if rel(s, t) == "diag"]))
             edges.append((m, t, cores[t], direct))
             edges += later
     return dict(rel=rel, pos=pos, team=team, relay=relay, todo=todo, proc=proc, edges=edges, mask_of=mask_of)
@@ -194,13 +196,13 @@ def rank_program(g, core, T, topo):
     d1, d2, tab = {}, {}, []
     if me is not None:
         pv0 = did(V.memset(T.pv[0:16, :], 0), "sv")
-        de = did(S.dma_start(out=T.e2[:], in_=T.end[:]), "de", 16)
         dm1 = did(Y.dma_start(out=T.m1[:], in_=T.idx[:]), "dm1", 16)
-        did(Y.dma_start(out=T.ei[0:16, :], in_=T.end[:]), "dp", 16)
-        wait(Y, pv0)
-        did(Y.dma_start(out=T.pv[1:16, :], in_=T.end[0:15, :]), "dp", 16)
-        dp = did(Y.dma_start(out=T.pv[0:1, 1:16], in_=T.end[15:16, 0:15]), "dp", 16)
         d1[me] = did(Y.dma_start(out=T.ix[0:16, me * 128:(me + 1) * 128], in_=T.idx[:]), "d1_%d" % me, 16)
+        de = did(S.dma_start(out=T.e2[:], in_=T.end[:]), "de", 16)
+        did(S.dma_start(out=T.ei[0:16, :], in_=T.end[:]), "dp", 16)
+        wait(S, pv0)
+        did(S.dma_start(out=T.pv[1:16, :], in_=T.end[0:15, :]), "dp", 16)
+        dp = did(S.dma_start(out=T.pv[0:1, 1:16], in_=T.end[15:16, 0:15]), "dp", 16)
         w, q = 128 // NL, R // NCH
         tab.append(did(S.dma_start(out=T.win[:, G:G + q], in_=T.tab[:, 0:q]), "tb0", 16))
         for k in range(NL):
@@ -220,11 +222,11 @@ def rank_program(g, core, T, topo):
         kid = did(g.affine_select(T.idn[0:16, :], T.ones[0:16, 0:16], [[1, 16]], A.is_equal, 0.0, 0, -1), "sg")
         krf = did(g.affine_select(T.repf[0:16, :], T.ones[0:16, :], [[0, 8], [1, 16]], A.is_equal, 0.0, 0, -1), "sg")
 
-    edges = [e for e in P["edges"] if e[2] == core]
+    mine = [[e for e in P["edges"] if e[:3] == (m, me, core)] for m in (1, 2)]
     exfree = None
     if me is not None:
         wait(g, dm1)
-        send(edges[0][3], [T.m1[:]], T.L1[me], "a1_%d" % me)
+        send(mine[0][0][3], [T.m1[:]], T.L1[me], "a1_%d" % me)
         wait(V, de)
         did(V.tensor_scalar(T.hl[:, 0:2], T.e2[:], 7, None, A.arith_shift_right), "sv")
         k = did(V.tensor_scalar(T.hl[:, 2:4], T.e2[:], 127, None, A.bitwise_and), "sv")
@@ -258,12 +260,12 @@ def rank_program(g, core, T, topo):
         wait(Y, k)
         k = did(Y.dma_start(out=T.m2[:], in_=T.mm[0:16, o:o + MW]), "dm2", 16)
         wait(g, k)
-        send(edges[1][3], [T.m2[:]], T.L2[me], "a2_%d" % me)
-    else:
-        for m, t, src, dsts in edges:
-            wait(g, arr[(m, t)])
-            L = (T.L1, T.L2)[m - 1]
-            send(dsts, [L[t]], L[t], "a%d_%d" % (m, t))
+        send(mine[1][0][3], [T.m2[:]], T.L2[me], "a2_%d" % me)
+    for m, t, src, dsts in P["edges"]:
+        if src != core or t == me: continue
+        wait(g, arr[(m, t)])
+        L = (T.L1, T.L2)[m - 1]
+        send(dsts, [L[t]], L[t], "a%d_%d" % (m, t))
     if nxt is not None:
         sw, w = [None, None], R // NCH
         for k in range(NCH):
@@ -280,12 +282,11 @@ def rank_program(g, core, T, topo):
         send([cores[t]], [blk("land", s) for s in ss], blk("land", ss[0]), "r_%d" % ss[0], op=2)
     if not lists: return finish()
 
-    for some in ([t for t in lists if rel(part, t) != "diag"], [t for t in lists if rel(part, t) == "diag"]):
-        for m, L, d, dst, w in ((1, T.L1, d1, "ix", 128), (2, T.L2, d2, "mm", MW)):
-            for t in some:
-                if t == me: continue
-                wait(Y, arr[(m, t)])
-                d[t] = did(Y.dma_start(out=T[dst][0:16, t * w:(t + 1) * w], in_=L[t]), "d%d_%d" % (m, t), 16)
+    for m, L, d, dst, w in ((1, T.L1, d1, "ix", 128), (2, T.L2, d2, "mm", MW)):
+        for t in sorted(lists, key=lambda t: rel(part, t) == "diag"):
+            if t == me: continue
+            wait(Y, arr[(m, t)])
+            d[t] = did(Y.dma_start(out=T[dst][0:16, t * w:(t + 1) * w], in_=L[t]), "d%d_%d" % (m, t), 16)
 
     wait(V, low)
     for ap in (T.win[:, 0:G], T.win[:, G + R:W], T.sc0[:, TL:SW], T.sc1[:, TL:SW]):
@@ -299,29 +300,26 @@ def rank_program(g, core, T, topo):
     vl = 0 if me is not None else min(n - 1, 1)
     steps = []
     for i in range(n):
-        if i == vl or i == n - 1: steps += [(i, 0, H), (i, H, Q), (i, H + Q, Q)]
+        if i == 0 and me is not None: steps += [(i, 0, H)]
+        elif n == 1: steps += [(i, k * Q, Q) for k in range(4)]
+        elif i == vl or i == n - 1: steps += [(i, 0, H), (i, H, Q), (i, H + Q, Q)]
         else: steps += [(i, 0, H), (i, H, H)]
+    if me is not None: steps += [(0, H, Q), (0, H + Q, Q)]
     vstep = steps.index((vl, H + Q, Q))
     first = [min(k for k in range(len(steps)) if steps[k][0] == i) for i in range(n)]
     final = [max(k for k in range(len(steps)) if steps[k][0] == i) for i in range(n)]
     mk = [T.mk0, T.mk1, T.mk2]
     free = {"rp": None, "ex": exfree}
-    v1, e1, v2, e2, v3, mtok, gtok, stok, scfree = {}, {}, {}, {}, {}, {}, {}, {}, {}
+    v2, e2, v3, mtok, gtok, stok, scfree = {}, {}, {}, {}, {}, {}, {}
 
-    def V1(i):
+    def offsets(i):
         t = lists[i]
         wait(V, d1[t])
-        v1[i] = did(V.tensor_scalar(T.cl[0:16, t * 128:(t + 1) * 128], T.ix[0:16, t * 128:(t + 1) * 128],
-                                    float(G - R * part), float(G + R), A.add, A.min), "sv")
-
-    def E1(i):
-        t = lists[i]
-        wait(E, v1[i], krf, free["rp"])
-        e1[i] = did(E.matmul(T.rp[:, 0:128], T.repf[0:16, :], T.cl[0:16, t * 128:(t + 1) * 128], True, True), "st")
-
-    def V2(i):
-        t = lists[i]
-        wait(V, e1[i])
+        k = did(V.tensor_scalar(T.cl[0:16, t * 128:(t + 1) * 128], T.ix[0:16, t * 128:(t + 1) * 128],
+                                float(G - R * part), float(G + R), A.add, A.min), "sv")
+        wait(E, k, krf, free["rp"])
+        k = did(E.matmul(T.rp[:, 0:128], T.repf[0:16, :], T.cl[0:16, t * 128:(t + 1) * 128], True, True), "st")
+        wait(V, k)
         v2[i] = free["rp"] = did(V.tensor_copy(T.offs[:, t * OW:t * OW + 128], T.rp[:, 0:128]), "sv")
 
     def E2(i):
@@ -383,9 +381,7 @@ def rank_program(g, core, T, topo):
         wait(g, k)
         return send([dest], [blk("res", t)], blk("land", part), "r_%d" % part)
 
-    V1(0)
-    E1(0)
-    V2(0)
+    offsets(0)
     for h in range(16):
         ksel = did(V.tensor_scalar(T.sel[0:16, h * 128:(h + 1) * 128], T.cst[0:16, :], T.idn[0:16, h:h + 1], None, A.mult), "sv")
     gather(0)
@@ -393,25 +389,17 @@ def rank_program(g, core, T, topo):
     E2(0)
     V3(0)
     if vl == 0: gather(vstep)
-    if n > 1:
-        V1(1)
-        E1(1)
-        V2(1)
+    for i in sorted(range(1, n), key=lambda i: rel(part, lists[i]) == "diag"): offsets(i)
     if vl == 1: gather(vstep)
     ahead, own = 1, None
     for k in range(len(steps)):
         i = steps[k][0]
-        while ahead < len(steps) and ahead <= k + 2 and steps[ahead][0] in v2:
+        while ahead < len(steps) and ahead <= k + 2:
             if ahead != vstep: gather(ahead)
             M(ahead)
-            if ahead == first[steps[ahead][0]]: E2(steps[ahead][0])
             ahead += 1
-        later = i + 1 if k == first[i] and i >= 1 and i + 1 < n else None
-        if later is not None:
-            V1(later)
-            E1(later)
+        if k == first[i] and i > 0: E2(i)
         scan(k)
-        if later is not None: V2(later)
         if k == first[i] and i > 0: V3(i)
         if k == final[i]:
             x = ext(i)
@@ -424,7 +412,7 @@ def rank_program(g, core, T, topo):
         s0 = [s for s in range(N) if rel(s, me) == "diag"][0]
         came[s0] = due("r_%d" % s0, bits(topo.mask(relay[me], core)))
         acc, ak = T.ex[:, 0:B], own
-        rest = sorted(came, key=lambda s: REST[P["pos"][me]].index((rel(s, me), P["pos"][s])))
+        rest = sorted(came, key=lambda s: REST[P["pos"][me]].index(rel(s, me)))
         for s in rest:
             wait(V, ak, came[s], free["ex"])
             ak = did(V.tensor_tensor(T.yb[:] if s == rest[-1] else acc, blk("land", s), blk("res", me) if s == rest[0] else acc,

from concourse.bass import DstId, RemoteDMATransfer
from concourse.mybir import AluOpType as A, ActivationFunctionType as AF

N, R, TL, B = 8, 4096, 2048, 256
ALL = 512
G = 4
W = R + 2 * G
H, Q = TL // 2, TL // 4
SW = TL + 4
OW = 144
MW = 160
NCH = 4
NL = 8
DEEP = 3
EARLY = 3
NG = 4

ORDER = {"o": [("own", 0), ("own", 1), ("diag", 0), ("diag", 1), ("cable", 0)],
         "h1": [("cable", 1), ("rack", 0), ("chip", 0), ("chip", 1)], "h2": [("rack", 1)], "h3": []}
REST = [["diag", "rack", "cable", "chip"], ["cable", "rack", "diag", "chip"]]

SCRATCH = {
    "win": ("sbuf", [128, W], "float32"),
    "gv": ("sbuf", [128, Q], "float32"),
    "sc0": ("sbuf", [128, SW], "float32"),
    "sc1": ("sbuf", [128, SW], "float32"),
    "sco": ("sbuf", [128, SW], "float32"),
    "res": ("sbuf", [128, N * B], "float32"),
    "land": ("sbuf", [128, N * B], "float32"),
    "yb": ("sbuf", [128, B], "float32"),
    "offs": ("sbuf", [128, N * OW], "uint16"),
    "ix": ("sbuf", [128, N * 128], "int32"),
    "cl": ("sbuf", [128, N * 128], "float32"),
    "mm": ("sbuf", [128, N * MW], "bfloat16"),
    "ones": ("sbuf", [128, 128], "float32"),
    "cst": ("sbuf", [128, 128], "bfloat16"),
    "iot": ("sbuf", [128, 128], "float32"),
    "idn": ("sbuf", [128, 16], "float32"),
    "repf": ("sbuf", [128, 128], "float32"),
    "rep1": ("sbuf", [128, 128], "bfloat16"),
    "rep16": ("sbuf", [128, 128], "bfloat16"),
    "sel": ("sbuf", [128, TL], "bfloat16"),
    "low": ("sbuf", [128, 4], "float32"),
    "e2": ("sbuf", [128, 2], "int32"),
    "hl": ("sbuf", [128, 4], "int32"),
    "hlf": ("sbuf", [128, 4], "float32"),
    "oh": ("sbuf", [128, 2 * OW], "bfloat16"),
    "ei": ("sbuf", [128, 16], "int32"),
    "pv": ("sbuf", [128, 16], "int32"),
    "ne": ("sbuf", [128, 16], "float32"),
    "eu": ("sbuf", [128, 16], "float32"),
    "ew": ("sbuf", [128, 16], "float32"),
    "exi": ("sbuf", [128, 16], "int32"),
    "xh": ("sbuf", [128, 32], "int32"),
    "m1": ("dram", [128, 16], "int32"),
    "m2": ("dram", [128, 20], "bfloat16"),
    "L1": ("dram", [N, 128, 16], "int32"),
    "L2": ("dram", [N, 128, 20], "bfloat16"),
    "mk0": ("psum", [128, H], "float32"),
    "mk1": ("psum", [128, H], "float32"),
    "mk2": ("psum", [128, H], "float32"),
    "rp": ("psum", [128, 512], "float32"),
    "ex": ("psum", [128, 512], "float32"),
}
for _k in range(NG): SCRATCH["gb%d" % _k] = ("sbuf", [128, H], "float32")
SEMAPHORES = (["sv", "ss", "st", "sg", "dm1", "dm2", "de", "dp", "snt", "sw0", "sw1", "dy"]
              + ["tb%d" % k for k in range(DEEP)] + ["tw%d" % k for k in range(NCH)]
              + ["%s_%d" % (n, t) for n in ("a1", "a2", "d1", "d2", "r") for t in range(N)])


def bits(m):
    return bin(m).count("1")


def the_plan(cores, topo):
    key = lambda c: (topo.host(c), topo.chip(c))
    chips = {}
    for c in range(ALL):
        chips.setdefault(key(c), []).append(c)
    mates = [[s for s in range(N) if key(cores[s]) == key(cores[t])] for t in range(N)]
    pos = [mates[t].index(t) for t in range(N)]

    def rel(s, t):
        a, b = cores[s], cores[t]
        if s == t: return "own"
        if key(a) == key(b): return "chip"
        if topo.host(a) != topo.host(b) and not topo.may_write(a, b): return "diag"
        return "rack" if topo.rack(topo.host(a)) == topo.rack(topo.host(b)) else "cable"

    team = []
    for s in range(N):
        free = [c for c in chips[key(cores[s])] if c not in cores]
        near = [c for c in free if topo.die(c) == topo.die(cores[s])]
        far = [c for c in free if topo.die(c) != topo.die(cores[s])]
        team.append({"o": cores[s], "h1": near[pos[s]], "h2": far[2 * pos[s]], "h3": far[2 * pos[s] + 1]})
    relay, via = [], [[], []]
    for t in range(N):
        across = team[[s for s in range(N) if rel(s, t) == "cable"][pos[t]]]
        relay.append(across["h3"])
        via[0].append(across["o"])
        via[1].append(across["h3"])
    todo, proc = {}, {}
    for s in range(N):
        for role in team[s]:
            lists = [t for k in ORDER[role] for t in range(N) if (rel(s, t), pos[t]) == k]
            todo[team[s][role]] = (s, lists)
            for t in lists: proc[(s, t)] = team[s][role]

    def mask_of(src, dsts):
        m = topo.mask(src, dsts[0])
        for d in dsts: m &= topo.mask(src, d)
        return m

    edges = []
    for m in (1, 2):
        for t in range(N):
            direct, later = [], []
            for k in ("cable", "rack", "chip"):
                pair = [proc[(s, t)] for s in range(N) if rel(s, t) == k]
                if len(pair) == 1 or pair[0] in cores:
                    direct += pair
                else:
                    i = (m + (k == "rack")) % 2
                    direct.append(pair[i])
                    later.append((m, t, pair[i], [pair[1 - i]]))
            v = via[m - 1][t]
            if v not in direct: direct.append(v)
            later.append((m, t, v, [proc[(s, t)] for s in range(N) if rel(s, t) == "diag"]))
            edges.append((m, t, cores[t], direct))
            edges += later
    return dict(rel=rel, pos=pos, team=team, relay=relay, todo=todo, proc=proc, edges=edges, mask_of=mask_of)


PLANS = {}


def rank_program(g, core, T, topo):
    cores = list(T.cores)
    if "p" not in PLANS: PLANS["p"] = the_plan(cores, topo)
    P = PLANS["p"]
    if core not in P["todo"]: return
    rel, relay, proc, mask_of = P["rel"], P["relay"], P["proc"], P["mask_of"]
    me = T.rank_of(core)
    V, S, E, Y = g.vector, g.scalar, g.tensor, g.sync
    cnt, seen, top = {}, {}, {}

    def due(sem, n):
        cnt[sem] = cnt.get(sem, 0) + n
        return (sem, cnt[sem])

    def wait(q, *toks):
        best = {}
        for k in toks:
            if k is not None: best[k[0]] = max(best.get(k[0], 0), k[1])
        name = "V" if q is V else "S" if q is S else "E" if q is E else "Y" if q is Y else "g"
        for sem in best:
            v = best[sem]
            if seen.get((name, sem), 0) < v:
                q.wait_ge(T.sem[sem], v)
                seen[(name, sem)] = v
                top[sem] = max(top.get(sem, 0), v)

    def did(ins, sem, n=1):
        ins.then_inc(T.sem[sem], n)
        return due(sem, n)

    def ids(dsts):
        out = []
        for d in dsts:
            rid, pid = topo.addr(d, core)
            out.append(DstId(rid=rid, pnc=pid))
        return out

    def send(dsts, srcs, dst, sem, local="snt", op=0):
        m = mask_of(core, dsts)
        g.remote_dma_fused([RemoteDMATransfer(dst_ids=ids(dsts), dma_engine_mask=m, remote_sem=T.sem[sem],
                                              srcs=srcs, dsts=[dst for d in dsts], alu_op=op)], local_sem=T.sem[local])
        return due(local, bits(m))

    def finish():
        for sem in cnt:
            if top.get(sem, 0) < cnt[sem]: wait(g, (sem, cnt[sem]))

    def blk(buf, t, w=B):
        return T[buf][:, t * w:(t + 1) * w]

    part, lists = P["todo"][core]
    team = P["team"][part]
    chain = [team[k] for k in ("o", "h1", "h2", "h3") if P["todo"][team[k]][1]]
    here = chain.index(core) if core in chain else len(chain)
    nxt = chain[here + 1] if here + 1 < len(chain) else None
    arr = {}
    for m, t, src, dsts in P["edges"]:
        if core in dsts: arr[(m, t)] = due("a%d_%d" % (m, t), bits(mask_of(src, dsts)))

    d1, d2, tab = {}, {}, []
    if me is not None:
        pv0 = did(V.memset(T.pv[0:16, :], 0), "sv")
        dm1 = did(Y.dma_start(out=T.m1[:], in_=T.idx[:]), "dm1", 16)
        d1[me] = did(Y.dma_start(out=T.ix[0:16, me * 128:(me + 1) * 128], in_=T.idx[:]), "d1_%d" % me, 16)
        de = did(S.dma_start(out=T.e2[:], in_=T.end[:]), "de", 16)
        did(S.dma_start(out=T.ei[0:16, :], in_=T.end[:]), "dp", 16)
        wait(S, pv0)
        did(S.dma_start(out=T.pv[1:16, :], in_=T.end[0:15, :]), "dp", 16)
        dp = did(S.dma_start(out=T.pv[0:1, 1:16], in_=T.end[15:16, 0:15]), "dp", 16)
        w, q = 128 // NL, R // NCH
        tab.append(did(S.dma_start(out=T.win[:, G:G + q], in_=T.tab[:, 0:q]), "tb0", 16))
        for k in range(NL):
            if k >= DEEP - 1: wait(S, tab[k + 1 - DEEP])
            tab.append(did(S.dma_start(out=T.win[k * w:(k + 1) * w, G + q:G + R], in_=T.tab[k * w:(k + 1) * w, q:R]),
                           "tb%d" % ((k + 1) % DEEP), 16))
    elif lists:
        tab = [due("tw%d" % k, bits(topo.mask(chain[here - 1], core))) for k in range(NCH)]

    if lists:
        k1 = did(V.memset(T.ones[:], 1.0), "sv")
        k2 = did(V.memset(T.cst[:], 1048576.0), "sv")
        low = did(V.memset(T.low[:], -9e29), "sv")
        did(V.memset(T.sco[:, TL:SW], 0.0), "sv")
        if me is not None: kio = did(g.iota(T.iot[:], [[1, 128]], 0, 0, allow_small_or_imprecise_dtypes=True), "sg")
        wait(g, k1)
        kid = did(g.affine_select(T.idn[0:16, :], T.ones[0:16, 0:16], [[1, 16]], A.is_equal, 0.0, 0, -1), "sg")
        krf = did(g.affine_select(T.repf[0:16, :], T.ones[0:16, :], [[0, 8], [1, 16]], A.is_equal, 0.0, 0, -1), "sg")

    mine = [[e for e in P["edges"] if e[:3] == (m, me, core)] for m in (1, 2)]
    exfree = None
    if me is not None:
        wait(g, dm1)
        send(mine[0][0][3], [T.m1[:]], T.L1[me], "a1_%d" % me)
        wait(V, de)
        did(V.tensor_scalar(T.hl[:, 0:2], T.e2[:], 7, None, A.arith_shift_right), "sv")
        k = did(V.tensor_scalar(T.hl[:, 2:4], T.e2[:], 127, None, A.bitwise_and), "sv")
        wait(V, k)
        k = did(V.tensor_copy(T.hlf[:], T.hl[:]), "sv")
        wait(V, k, kio)
        for h in range(2):
            o = h * OW
            did(V.tensor_scalar(T.oh[:, o:o + 16], T.iot[:, 0:16], T.hlf[:, h:h + 1], None, A.is_equal), "sv")
            k = did(V.tensor_scalar(T.oh[:, o + 16:o + OW], T.iot[:], T.hlf[:, 2 + h:3 + h], None, A.is_equal), "sv")
        wait(E, k)
        for h in range(2):
            o = h * OW
            kf = did(E.matmul(T.ex[0:16, 0:128], T.oh[:, o:o + 16], T.oh[:, o + 16:o + OW], h == 0, h == 1), "st")
        wait(V, dp)
        did(V.tensor_tensor(T.ne[0:16, :], T.ei[0:16, :], T.pv[0:16, :], A.is_gt), "sv")
        k = did(V.tensor_scalar(T.eu[0:16, :], T.ei[0:16, :], float(-1 - TL), None, A.add), "sv")
        wait(V, k)
        k = did(V.tensor_tensor(T.ew[0:16, :], T.eu[0:16, :], T.ne[0:16, :], A.mult), "sv")
        wait(V, k)
        k = did(V.tensor_scalar(T.exi[0:16, :], T.ew[0:16, :], float(TL), None, A.add), "sv")
        wait(V, k)
        did(V.tensor_scalar(T.xh[0:16, 0:16], T.exi[0:16, :], 4, None, A.arith_shift_right), "sv")
        k = did(V.tensor_scalar(T.xh[0:16, 16:32], T.exi[0:16, :], 15, None, A.bitwise_and), "sv")
        wait(V, k)
        o = me * MW
        did(V.tensor_copy(T.mm[0:16, o + 128:o + MW], T.xh[0:16, :]), "sv")
        wait(V, kf)
        k = did(V.tensor_scalar(T.mm[0:16, o:o + 128], T.ex[0:16, 0:128], -2.0 ** 90, 2.0 ** 89, A.mult, A.add), "sv")
        exfree = d2[me] = k
        wait(Y, k)
        k = did(Y.dma_start(out=T.m2[:], in_=T.mm[0:16, o:o + MW]), "dm2", 16)
        wait(g, k)
        send(mine[1][0][3], [T.m2[:]], T.L2[me], "a2_%d" % me)
    for m, t, src, dsts in P["edges"]:
        if src != core or t == me: continue
        wait(g, arr[(m, t)])
        L = (T.L1, T.L2)[m - 1]
        send(dsts, [L[t]], L[t], "a%d_%d" % (m, t))
    if nxt is not None:
        sw, w = [None, None], R // NCH
        for k in range(NCH):
            if me is None: wait(g, tab[k])
            elif k == 0: wait(g, *tab[:len(tab) - EARLY])
            else: wait(g, *tab)
            wait(g, sw[k % 2])
            piece = T.win[:, G + k * w:G + (k + 1) * w]
            sw[k % 2] = send([nxt], [piece], piece, "tw%d" % k, "sw%d" % (k % 2))
    for t in range(N):
        if relay[t] != core: continue
        ss = [s for s in range(N) if rel(s, t) == "diag"]
        wait(g, *[due("r_%d" % s, bits(topo.mask(proc[(s, t)], core))) for s in ss])
        send([cores[t]], [blk("land", s) for s in ss], blk("land", ss[0]), "r_%d" % ss[0], op=2)
    if not lists: return finish()

    for m, L, d, dst, w in ((1, T.L1, d1, "ix", 128), (2, T.L2, d2, "mm", MW)):
        for t in sorted(lists, key=lambda t: rel(part, t) == "diag"):
            if t == me: continue
            wait(Y, arr[(m, t)])
            d[t] = did(Y.dma_start(out=T[dst][0:16, t * w:(t + 1) * w], in_=L[t]), "d%d_%d" % (m, t), 16)

    wait(V, low)
    for ap in (T.win[:, 0:G], T.win[:, G + R:W], T.sc0[:, TL:SW], T.sc1[:, TL:SW]):
        kgd = did(V.tensor_scalar(ap, T.low[:], 4.0, None, A.mult), "sv")
    wait(V, k2, kid, krf)
    did(V.tensor_copy(T.rep1[0:16, :], T.repf[0:16, :]), "sv")
    krp = did(V.tensor_scalar(T.rep16[0:16, :], T.repf[0:16, :], 16.0, None, A.mult), "sv")
    ksel = None

    n = len(lists)
    vl = 0 if me is not None else min(n - 1, 1)
    steps = []
    for i in range(n):
        if i == 0 and me is not None: steps += [(i, 0, H)]
        elif n == 1: steps += [(i, k * Q, Q) for k in range(4)]
        elif i == vl or i == n - 1: steps += [(i, 0, H), (i, H, Q), (i, H + Q, Q)]
        else: steps += [(i, 0, H), (i, H, H)]
    if me is not None: steps += [(0, H, Q), (0, H + Q, Q)]
    vstep = steps.index((vl, H + Q, Q))
    first = [min(k for k in range(len(steps)) if steps[k][0] == i) for i in range(n)]
    final = [max(k for k in range(len(steps)) if steps[k][0] == i) for i in range(n)]
    mk = [T.mk0, T.mk1, T.mk2]
    free = {"rp": None, "ex": exfree}
    v2, e2, v3, mtok, gtok, stok, scfree = {}, {}, {}, {}, {}, {}, {}

    def offsets(i):
        t = lists[i]
        wait(V, d1[t])
        k = did(V.tensor_scalar(T.cl[0:16, t * 128:(t + 1) * 128], T.ix[0:16, t * 128:(t + 1) * 128],
                                float(G - R * part), float(G + R), A.add, A.min), "sv")
        wait(E, k, krf, free["rp"])
        k = did(E.matmul(T.rp[:, 0:128], T.repf[0:16, :], T.cl[0:16, t * 128:(t + 1) * 128], True, True), "st")
        wait(V, k)
        v2[i] = free["rp"] = did(V.tensor_copy(T.offs[:, t * OW:t * OW + 128], T.rp[:, 0:128]), "sv")

    def E2(i):
        o = lists[i] * MW
        wait(E, d2[lists[i]], krp, free["ex"])
        did(E.matmul(T.ex[:, 0:16], T.rep16[0:16, :], T.mm[0:16, o + 128:o + 144], True, False), "st")
        e2[i] = did(E.matmul(T.ex[:, 0:16], T.rep1[0:16, :], T.mm[0:16, o + 144:o + 160], False, True), "st")

    def V3(i):
        o = lists[i] * OW
        wait(V, e2[i])
        v3[i] = free["ex"] = did(V.tensor_copy(T.offs[:, o + 128:o + OW], T.ex[:, 0:16]), "sv")

    def M(k):
        i, a, w = steps[k]
        o = lists[i] * MW
        wait(E, d2[lists[i]], ksel, stok.get(k - 3))
        for h in range(w // 128):
            hh = a // 128 + h
            mtok[k] = did(E.matmul(mk[k % 3][:, h * 128:(h + 1) * 128], T.sel[0:16, hh * 128:(hh + 1) * 128],
                                   T.mm[0:16, o:o + 128], True, True), "st")

    def gathered(k):
        return T.gv if k == vstep else T["gb%d" % (k % NG)]

    def gather(k):
        i, a, w = steps[k]
        o = lists[i] * OW + a // 16
        from_win = T.win[:, :].indirect(T.offs[:, o:o + w // 16])
        if k == vstep:
            wait(V, v2[i], kgd, *tab)
            gtok[k] = did(V.tensor_copy(T.gv[:, 0:w], from_win), "sv")
        else:
            wait(S, v2[i], kgd, stok.get(k - NG), *tab)
            gtok[k] = did(S.activation(gathered(k)[:, 0:w], from_win, AF.Copy), "ss")

    def scbuf(i):
        return "sco" if lists[i] == part else "sc%d" % (i % 2)

    def scan(k):
        i, a, w = steps[k]
        sc = T[scbuf(i)]
        before = [stok[j] for j in range(k) if steps[j][0] == i][-1:]
        wait(V, mtok[k], gtok[k], kgd, scfree.get(scbuf(i)), *before)
        init = sc[:, a - 1:a] if a else T.win[:, 0:1]
        stok[k] = did(V.tensor_tensor_scan(sc[:, a:a + w], mk[k % 3][:, 0:w], gathered(k)[:, 0:w], init, A.min, A.max), "sv")

    def picked(i):
        o = lists[i] * OW
        return T[scbuf(i)][:, :].indirect(T.offs[:, o + 128:o + OW])

    def ext(i):
        t = lists[i]
        wait(V, stok[final[i]], v3[i])
        k = did(V.tensor_copy(blk("res", t), picked(i)), "sv")
        scfree[scbuf(i)] = k
        if t == me: return k
        dest = relay[t] if rel(part, t) == "diag" else cores[t]
        wait(g, k)
        return send([dest], [blk("res", t)], blk("land", part), "r_%d" % part)

    offsets(0)
    for h in range(16):
        ksel = did(V.tensor_scalar(T.sel[0:16, h * 128:(h + 1) * 128], T.cst[0:16, :], T.idn[0:16, h:h + 1], None, A.mult), "sv")
    gather(0)
    M(0)
    E2(0)
    V3(0)
    if vl == 0: gather(vstep)
    for i in sorted(range(1, n), key=lambda i: rel(part, lists[i]) == "diag"): offsets(i)
    if vl == 1: gather(vstep)
    ahead, own = 1, None
    for k in range(len(steps)):
        i = steps[k][0]
        while ahead < len(steps) and ahead <= k + 2:
            if ahead != vstep: gather(ahead)
            M(ahead)
            ahead += 1
        if k == first[i] and i > 0: E2(i)
        scan(k)
        if k == first[i] and i > 0: V3(i)
        if k == final[i]:
            x = ext(i)
            if lists[i] == me: own = x

    if me is not None:
        came = {}
        for s in range(N):
            if s != me and rel(s, me) != "diag": came[s] = due("r_%d" % s, bits(topo.mask(proc[(s, me)], core)))
        s0 = [s for s in range(N) if rel(s, me) == "diag"][0]
        came[s0] = due("r_%d" % s0, bits(topo.mask(relay[me], core)))
        acc, ak = T.ex[:, 0:B], own
        rest = sorted(came, key=lambda s: REST[P["pos"][me]].index(rel(s, me)))
        for s in rest:
            wait(V, ak, came[s], free["ex"])
            ak = did(V.tensor_tensor(T.yb[:] if s == rest[-1] else acc, blk("land", s), blk("res", me) if s == rest[0] else acc,
                                     A.max), "sv")
        wait(Y, ak)
        did(Y.dma_start(out=T.y[:], in_=T.yb[:]), "dy", 16)
    finish()
